import numpy as np
import ml_dtypes


def mxq(x, axis, fmt="e4m3"):
    dtype, down = {"e4m3": (ml_dtypes.float8_e4m3fn, 7), "e5m2": (ml_dtypes.float8_e5m2, 14)}[fmt]
    v = np.moveaxis(np.asarray(x, np.float32).astype(ml_dtypes.bfloat16).astype(np.float64), axis, -1)
    blocks = v.reshape(v.shape[:-1] + (-1, 32))
    amax = np.abs(blocks).max(-1, keepdims=True)
    byte = np.maximum(np.where(amax > 0, np.frexp(amax)[1] - 1 + 127, 0) - down, 1)
    scale = np.exp2(byte - 127.0)
    codes = (blocks / scale).astype(np.float32).astype(dtype).astype(np.float64)
    return np.moveaxis((codes * scale).reshape(v.shape), -1, axis)


WIDE = False


def mx_kscale(k):
    if not WIDE:
        return np.ones(k)
    levels = np.array([10, -10, 5, -5, 0])
    if k % 512:
        return np.exp2(np.random.permutation(np.resize(levels, k // 32))).repeat(32)
    a = np.empty((k // 512, 16))
    for p in range(k // 512):
        a[p, :8] = np.random.permutation(np.resize(levels, 8))
        for g in range(8):
            far = levels[np.abs(levels - a[p, g]) >= 10]
            a[p, g + 8] = far[np.random.randint(len(far))]
    return np.exp2(a.ravel()).repeat(32)


def f64(x):
    return np.asarray(x).astype(np.float64)


def striped(idx):
    return np.tile(idx.reshape(-1, 16).T, (8, 1)).astype(np.uint16)


def unstriped(offs):
    return offs[:16].T.reshape(-1).astype(np.int64)


def striped8(idx):
    return np.concatenate([x.reshape(-1, 16).T for x in idx]).astype(np.uint16)


def runs(offs, k):
    lists = np.stack([offs[16 * r : 16 * r + 16].T.reshape(-1) for r in range(8)]).astype(np.int64)
    return lists[np.arange(k) % 512 // 64]


def pack_weight(w):
    k, n = w.shape
    w = f64(np.asarray(w, np.float32).astype(ml_dtypes.bfloat16)).reshape(k // 32, 32, n)
    amax = np.abs(w).max(1)
    byte = np.clip(np.where(amax > 0, np.frexp(amax)[1] - 1 + 127 - 7, 1), 1, 254)
    scaled = (w * np.exp2(127.0 - byte)[:, None, :]).reshape(k, n).astype(np.float32)
    words = np.ascontiguousarray(scaled.reshape(k // 512, 128, 4, n).transpose(0, 1, 3, 2)).astype(ml_dtypes.float8_e4m3fn).view(np.uint8)
    return words, np.ascontiguousarray(byte.astype(np.uint8).reshape(k // 512, 16, n))


def unpack_weight(words, scales):
    g, p, n, _ = words.shape
    vals = np.ascontiguousarray(words).view(ml_dtypes.float8_e4m3fn).astype(np.float64) * np.repeat(np.exp2(scales.astype(np.float64) - 127.0), 8, axis=1)[..., None]
    return vals.transpose(0, 1, 3, 2).reshape(g * 512, n)


def relu(v):
    return np.maximum(v, 0.0)

def planes(y):
    n, m = y.shape
    v = y.astype(np.float32).astype(ml_dtypes.bfloat16).astype(np.float64).reshape(n // 32, 32, m)
    top = np.abs(v).max(1)
    byte = np.clip(np.where(top > 0, np.frexp(top)[1] - 1 + 127 - 7, 1), 1, 254)
    codes = (v * np.exp2(127.0 - byte)[:, None, :]).reshape(n, m).astype(np.float32).astype(ml_dtypes.float8_e4m3fn).view(np.uint8)
    words = codes.reshape(n // 512, 128, 4, m).transpose(0, 1, 3, 2)
    return np.ascontiguousarray(words), np.ascontiguousarray(byte.astype(np.uint8).reshape(n // 512, 16, m))


K, T, S, N, G, H, W = 512, 1024, 512, 512, 2048, 512, 384


def setup_inputs():
    n = np.random.standard_normal
    s = mx_kscale(K)[:, None]
    u = mx_kscale(S)
    packed_xT = pack_weight(n((K, T)) * s)
    packed_dT = pack_weight(n((K, G)) / s)
    packed_w1 = pack_weight(n((H, N)) / np.sqrt(2 * H) / u[:, None])
    packed_w2 = pack_weight(n((K, N)) / np.sqrt(2 * K) / s)
    return {
        "x_words": packed_xT[0],
        "x_scales": packed_xT[1],
        "d_words": packed_dT[0],
        "d_scales": packed_dT[1],
        "gn": (np.random.uniform(0.5, 1.5, (H, 1)) * u[:, None]).astype(np.float32),
        "w1_words": packed_w1[0],
        "w1_scales": packed_w1[1],
        "w2_words": packed_w2[0],
        "w2_scales": packed_w2[1],
        "offs": striped(np.random.permutation(T)[:S]),
        "k1": striped8(np.random.randint(0, G, (8, H))),
        "n1": striped8(np.stack([np.random.permutation(S) for _ in range(8)])),
        "n2": striped8(np.stack([np.random.permutation(S) for _ in range(8)])),
        "two": striped(np.random.permutation(T)[:S]),
        "n3": striped(np.random.permutation(S)[:W]),
        "n4": striped(np.random.permutation(S)[:W]),
    }


def reference(x_words, x_scales, d_words, d_scales, gn, w1_words, w1_scales, w2_words, w2_scales, offs, k1, n1, n2, two, n3, n4):
    d_k1 = unpack_weight(d_words, d_scales)[np.arange(K)[:, None], runs(k1, K)]
    xq = unpack_weight(x_words, x_scales)[:, unstriped(offs)]
    h = 0.0625 * (d_k1.T @ xq)
    pa = h - (h[np.arange(H)[:, None], runs(n1, H)])
    pb = h[np.arange(H)[:, None], runs(n2, H)] - h
    z = f64(gn) * (relu(np.minimum(pa, pb)) - (relu(-1.0 * np.maximum(pa, pb))))
    x_two = unpack_weight(x_words, x_scales)[:, unstriped(two)]
    h2 = unpack_weight(w1_words, w1_scales).T @ mxq(z, 0, "e4m3") + unpack_weight(w2_words, w2_scales).T @ x_two
    old = h2[:, unstriped(n3)]
    pa2 = h2[:, unstriped(n4)]
    ra = old - (0.5 * pa2)
    out = h2.copy()
    out[:, unstriped(n3)] = ra
    return (out,) + planes(out)

@@ -1,0 +1,251 @@
+from contextlib import ExitStack
+
+import concourse.mybir as mybir
+
+F32 = mybir.dt.float32
+BF16 = mybir.dt.bfloat16
+I32 = mybir.dt.int32
+U32 = mybir.dt.uint32
+U16 = mybir.dt.uint16
+U8 = mybir.dt.uint8
+FP8X4 = mybir.dt.float8_e4m3fn_x4
+ALU = mybir.AluOpType
+COPY = mybir.ActivationFunctionType.Copy
+
+K, T, S, N, G, H, W = 512, 1024, 512, 512, 2048, 512, 384
+P = 128
+PACK = 4
+FLOPS = 3 * 2 * 512 * 512 * 512
+CHUNKS = ((0, 256), (256, 512))
+
+
+def tile_picked_pqmixminmodkdif_none_po_kernel(
+    tc, x_words, x_scales, d_words, d_scales, gn, w1_words, w1_scales, w2_words, w2_scales,
+    offs, k1, n1, n2, two, n3, n4, out_0, out_1, out_2,
+):
+    nc = tc.nc
+
+    def words_of(dram):
+        return dram[0].rearrange("p n t -> p (n t)").bitcast(I32)
+
+    with ExitStack() as ctx:
+        lists = ctx.enter_context(tc.tile_pool(name="lists", bufs=1))
+        keep = ctx.enter_context(tc.tile_pool(name="keep", bufs=1))
+        psum = ctx.enter_context(tc.psum_pool(name="psum", bufs=1))
+
+        def tile(name, shape, dtype):
+            return keep.tile(shape, dtype, name=name, align_bytes=64)
+
+        def load_list(name, dram):
+            held = lists.tile(list(dram.shape), U16, name=name)
+            nc.sync.dma_start(held[:], dram)
+            return held
+
+        def load_scale_rows(queue, plane, first_row, dram):
+            for q in range(4):
+                queue.dma_start(
+                    out=plane[32 * q + first_row : 32 * q + first_row + 4, :].bitcast(I32),
+                    in_=dram[0, 4 * q : 4 * q + 4, :].bitcast(I32),
+                )
+
+        def deal(dealt, plain):
+            nc.vector.tensor_copy(
+                out=dealt.rearrange("p (t m) -> p m t", t=PACK),
+                in_=plain.rearrange("p (m t) -> p m t", t=PACK),
+            )
+
+        d_scale_table = tile("d_scale_table", [P, G], U8)
+        x_scale_table = tile("x_scale_table", [P, T], U8)
+        d_plane = tile("d_plane", [P, H], U8)
+        w_plane_plain = tile("w_plane_plain", [P, N], U8)
+        nc.gpsimd.memset(d_scale_table[:].bitcast(I32), 0)
+        nc.vector.memset(x_scale_table[:].bitcast(I32), 0)
+        nc.gpsimd.memset(d_plane[:].bitcast(I32), 0)
+        nc.gpsimd.memset(w_plane_plain[:].bitcast(I32), 0)
+
+        k1_list = load_list("k1_list", k1)
+        nc.sync.dma_start(out=d_scale_table[0:P:8, :].bitcast(I32), in_=d_scales[0].bitcast(I32))
+        offs_list = load_list("offs_list", offs)
+        d_table = tile("d_table", [P, G], U32)
+        nc.sync.dma_start(out=d_table[:].bitcast(I32), in_=words_of(d_words))
+        x_table = tile("x_table", [P, T], U32)
+        nc.sync.dma_start(out=x_table[:].bitcast(I32), in_=words_of(x_words))
+        load_scale_rows(nc.scalar, x_scale_table, 0, x_scales)
+        two_list = load_list("two_list", two)
+        gain = tile("gain", [P, PACK], F32)
+        nc.sync.dma_start(out=gain[:], in_=gn.rearrange("(p t) o -> p (t o)", t=PACK))
+        n1_list = load_list("n1_list", n1)
+        n2_list = load_list("n2_list", n2)
+        w1_plain = tile("w1_plain", [P, N], U32)
+        w2_plain = tile("w2_plain", [P, N], U32)
+        nc.sync.dma_start(out=w2_plain[:].bitcast(I32), in_=words_of(w2_words))
+        nc.sync.dma_start(out=w1_plain[:].bitcast(I32), in_=words_of(w1_words))
+        load_scale_rows(nc.sync, w_plane_plain, 4, w2_scales)
+        load_scale_rows(nc.sync, w_plane_plain, 0, w1_scales)
+        n4_list = load_list("n4_list", n4)
+        n3_list = load_list("n3_list", n3)
+
+        d_bytes = tile("d_bytes", [P, H], U8)
+        nc.vector.tensor_copy(d_bytes[:], d_scale_table[:].indirect(k1_list[:]))
+        d_bytes_dealt = tile("d_bytes_dealt", [P, H], U8)
+        deal(d_bytes_dealt[:], d_bytes[:])
+        for j in range(4):
+            nc.scalar.dma_start(
+                out=d_plane[j:P:32, :].bitcast(I32), in_=d_bytes_dealt[8 * j : P : 32, :].bitcast(I32)
+            )
+        x_plane = tile("x_plane", [P, S], U8)
+        nc.vector.tensor_copy(x_plane[:], x_scale_table[:].indirect(offs_list[:]))
+        d_picked = tile("d_picked", [P, H], U32)
+        nc.vector.tensor_copy(d_picked[:], d_table[:].indirect(k1_list[:]))
+        d_codes = tile("d_codes", [P, H], U32)
+        deal(d_codes[:], d_picked[:])
+
+        scaled_gain = tile("scaled_gain", [P, PACK], F32)
+        nc.gpsimd.tensor_scalar(scaled_gain[:], gain[:], 0.0625, 0.0, ALU.mult, ALU.add)
+
+        h_rows = [tile("h_rows%d" % t, [P, S], F32) for t in range(PACK)]
+        for c, (lo, hi) in enumerate(CHUNKS):
+            x_codes = tile("x_codes%d" % c, [P, hi - lo], U32)
+            nc.vector.tensor_copy(x_codes[:], x_table[:].indirect(offs_list[:, lo // 16 : hi // 16]))
+            for t in range(PACK):
+                cols = slice(P * t, P * (t + 1))
+                bank = psum.tile([P, hi - lo], F32, name="h_bank%d_%d" % (c, t), tag="bank%d" % (PACK * c + t))
+                nc.tensor.matmul_mx(
+                    out=bank[:], lhsT=d_codes[:, cols].bitcast(FP8X4), lhsT_scale=d_plane[:, cols],
+                    rhs=x_codes[:].bitcast(FP8X4), rhs_scale=x_plane[:, lo:hi], start=True, stop=True,
+                )
+                nc.scalar.activation(h_rows[t][:, lo:hi], bank[:], COPY, scale=scaled_gain[:, t : t + 1])
+
+        two_codes = tile("two_codes", [P, S], U32)
+        nc.vector.tensor_copy(two_codes[:], x_table[:].indirect(two_list[:]))
+        two_plane = tile("two_plane", [P, S], U8)
+        nc.vector.tensor_copy(two_plane[:], x_scale_table[:].indirect(two_list[:]))
+        w1_codes = tile("w1_codes", [P, N], U32)
+        w2_codes = tile("w2_codes", [P, N], U32)
+        w_plane = tile("w_plane", [P, N], U8)
+        deal(w2_codes[:], w2_plain[:])
+        deal(w_plane[:], w_plane_plain[:])
+        deal(w1_codes[:], w1_plain[:])
+
+        h2_rows = [tile("h2_rows%d" % t, [P, S], F32) for t in range(PACK)]
+        h2_banks = []
+        for c, (lo, hi) in enumerate(CHUNKS):
+            n = hi - lo
+            picks = slice(lo // 16, hi // 16)
+            at_n1 = tile("at_n1_%d" % c, [P, PACK, n], F32)
+            at_n2 = tile("at_n2_%d" % c, [P, PACK, n], F32)
+            pa = tile("pa%d" % c, [P, PACK, n], F32)
+            pb = tile("pb%d" % c, [P, PACK, n], F32)
+            for t in range(PACK):
+                nc.scalar.activation(at_n1[:, t, :], h_rows[t][:].indirect(n1_list[:, picks]), COPY)
+                nc.scalar.activation(at_n2[:, t, :], h_rows[t][:].indirect(n2_list[:, picks]), COPY)
+                nc.vector.tensor_tensor(pa[:, t, :], h_rows[t][:, lo:hi], at_n1[:, t, :], ALU.subtract)
+                nc.vector.tensor_tensor(pb[:, t, :], at_n2[:, t, :], h_rows[t][:, lo:hi], ALU.subtract)
+            capped = tile("capped%d" % c, [P, PACK, n], F32)
+            z_pairs = tile("z_pairs%d" % c, [P, 2, n, 2], BF16)
+            for u in range(2):
+                pair = slice(2 * u, 2 * u + 2)
+                nc.vector.scalar_tensor_tensor(
+                    capped[:, pair, :], pb[:, pair, :], 0.0, pa[:, pair, :], ALU.max, ALU.min
+                )
+                nc.vector.scalar_tensor_tensor(
+                    z_pairs[:, u, :, :], pb[:, pair, :].rearrange("p e j -> p j e"), 0.0,
+                    capped[:, pair, :].rearrange("p e j -> p j e"), ALU.min, ALU.max,
+                )
+            z_grouped = tile("z_grouped%d" % c, [P, n * PACK], BF16)
+            nc.vector.tensor_copy(
+                out=z_grouped[:].bitcast(F32).rearrange("p (j u) -> p j u", u=2),
+                in_=z_pairs[:].rearrange("p u j e -> p (u j e)").bitcast(F32).rearrange("p (u j) -> p j u", u=2),
+            )
+            z_codes = tile("z_codes%d" % c, [P, n], U32)
+            z_plane = tile("z_plane%d" % c, [P, n], U8)
+            nc.vector.quantize_mx(out=z_codes[:].bitcast(FP8X4), scales=z_plane[:], in_=z_grouped[:])
+            banks = []
+            for t in range(PACK):
+                cols = slice(P * t, P * (t + 1))
+                bank = psum.tile([P, n], F32, name="h2_bank%d_%d" % (c, t), tag="bank%d" % (PACK * c + t))
+                nc.tensor.matmul_mx(
+                    out=bank[:], lhsT=w2_codes[:, cols].bitcast(FP8X4), lhsT_scale=w_plane[4:P, cols],
+                    rhs=two_codes[:, lo:hi].bitcast(FP8X4), rhs_scale=two_plane[:, lo:hi], start=True, stop=False,
+                )
+                banks.append(bank)
+            for t in (0, 1, 3, 2):
+                cols = slice(P * t, P * (t + 1))
+                nc.tensor.matmul_mx(
+                    out=banks[t][:], lhsT=w1_codes[:, cols].bitcast(FP8X4), lhsT_scale=w_plane[:, cols],
+                    rhs=z_codes[:].bitcast(FP8X4), rhs_scale=z_plane[:], start=False, stop=True,
+                )
+            h2_banks.append(banks)
+
+        def leave_psum(c, t):
+            lo, hi = CHUNKS[c]
+            nc.scalar.copy(h2_rows[t][:, lo:hi], h2_banks[c][t][:])
+
+        def leave_psum_vector(c, t):
+            lo, hi = CHUNKS[c]
+            nc.vector.tensor_copy(h2_rows[t][:, lo:hi], h2_banks[c][t][:])
+
+        old = [tile("old%d" % t, [P, W], F32) for t in range(PACK)]
+        pull = [tile("pull%d" % t, [P, W], F32) for t in range(PACK)]
+        out_pairs = tile("out_pairs", [P, 2, S, 2], BF16)
+        out_rows = out_0.rearrange("(p t) j -> p t j", t=PACK)
+
+        def fetch_pull(t):
+            nc.scalar.activation(pull[t][:], h2_rows[t][:].indirect(n4_list[:]), COPY, scale=-0.5)
+
+        def scatter_sum(t):
+            for lo in range(0, W, W // 2):
+                hi = lo + W // 2
+                nc.vector.tensor_tensor(
+                    h2_rows[t][:].indirect(n3_list[:, lo // 16 : hi // 16]), old[t][:, lo:hi], pull[t][:, lo:hi], ALU.add
+                )
+            nc.sync.dma_start(out=out_rows[:, t, :], in_=h2_rows[t][:])
+
+        def fetch_sum(t):
+            nc.vector.tensor_tensor(old[t][:], h2_rows[t][:].indirect(n3_list[:]), pull[t][:], ALU.add)
+
+        def scatter_copy(t):
+            nc.scalar.activation(h2_rows[t][:].indirect(n3_list[:]), old[t][:], COPY)
+            nc.sync.dma_start(out=out_rows[:, t, :], in_=h2_rows[t][:])
+
+        def round_rows(t):
+            nc.vector.tensor_copy(out=out_pairs[:, t // 2, :, t % 2], in_=h2_rows[t][:])
+
+        last = len(CHUNKS) - 1
+        for c in range(last):
+            for t in range(PACK):
+                leave_psum(c, t)
+        leave_psum(last, 0)
+        leave_psum_vector(last, 1)
+        nc.vector.tensor_copy(old[0][:], h2_rows[0][:].indirect(n3_list[:]))
+        fetch_pull(1)
+        fetch_pull(0)
+        fetch_sum(1)
+        scatter_sum(0)
+        leave_psum(last, 3)
+        fetch_pull(3)
+        leave_psum(last, 2)
+        scatter_copy(1)
+        fetch_sum(3)
+        round_rows(0)
+        fetch_pull(2)
+        nc.vector.tensor_copy(old[2][:], h2_rows[2][:].indirect(n3_list[:]))
+        scatter_copy(3)
+        scatter_sum(2)
+        for t in (1, 2, 3):
+            round_rows(t)
+
+        out_grouped = tile("out_grouped", [P, S * PACK], BF16)
+        nc.vector.tensor_copy(
+            out=out_grouped[:].bitcast(F32).rearrange("p (j u) -> p j u", u=2),
+            in_=out_pairs[:].rearrange("p u j e -> p (u j e)").bitcast(F32).rearrange("p (u j) -> p j u", u=2),
+        )
+        out_codes = tile("out_codes", [P, S], U32)
+        out_plane = tile("out_plane", [P, S], U8)
+        nc.vector.quantize_mx(out=out_codes[:].bitcast(FP8X4), scales=out_plane[:], in_=out_grouped[:])
+        nc.sync.dma_start(out=words_of(out_1), in_=out_codes[:].bitcast(I32))
+        for q in range(4):
+            queue = nc.scalar if q % 2 == 0 else nc.sync
+            queue.dma_start(
+                out=out_2[0, 4 * q : 4 * q + 4, :].bitcast(I32), in_=out_plane[32 * q : 32 * q + 4, :].bitcast(I32)
+            )

@@ -17,6 +17,8 @@ P = 128
 PACK = 4
 FLOPS = 3 * 2 * 512 * 512 * 512
 CHUNKS = ((0, 256), (256, 512))
+FUSED = 0
+SPLIT = 384
 
 
 def tile_picked_pqmixminmodkdif_none_po_kernel(
@@ -33,8 +35,8 @@ def tile_picked_pqmixminmodkdif_none_po_kernel(
         keep = ctx.enter_context(tc.tile_pool(name="keep", bufs=1))
         psum = ctx.enter_context(tc.psum_pool(name="psum", bufs=1))
 
-        def tile(name, shape, dtype):
-            return keep.tile(shape, dtype, name=name, align_bytes=64)
+        def tile(name, shape, dtype, tag=None):
+            return keep.tile(shape, dtype, name=name, tag=tag or name, align_bytes=64)
 
         def load_list(name, dram):
             held = lists.tile(list(dram.shape), U16, name=name)
@@ -56,138 +58,198 @@ def tile_picked_pqmixminmodkdif_none_po_kernel(
 
         d_scale_table = tile("d_scale_table", [P, G], U8)
         x_scale_table = tile("x_scale_table", [P, T], U8)
-        d_plane = tile("d_plane", [P, H], U8)
-        w_plane_plain = tile("w_plane_plain", [P, N], U8)
         nc.gpsimd.memset(d_scale_table[:].bitcast(I32), 0)
         nc.vector.memset(x_scale_table[:].bitcast(I32), 0)
-        nc.gpsimd.memset(d_plane[:].bitcast(I32), 0)
-        nc.gpsimd.memset(w_plane_plain[:].bitcast(I32), 0)
 
         k1_list = load_list("k1_list", k1)
-        nc.sync.dma_start(out=d_scale_table[0:P:8, :].bitcast(I32), in_=d_scales[0].bitcast(I32))
         offs_list = load_list("offs_list", offs)
+        for e in range(2):
+            nc.sync.dma_start(out=d_scale_table[e:P:16, :].bitcast(I32), in_=d_scales[0, e:16:2, :].bitcast(I32))
         d_table = tile("d_table", [P, G], U32)
-        nc.sync.dma_start(out=d_table[:].bitcast(I32), in_=words_of(d_words))
         x_table = tile("x_table", [P, T], U32)
+        nc.sync.dma_start(out=d_table[:].bitcast(I32), in_=words_of(d_words))
+        load_scale_rows(nc.sync, x_scale_table, 0, x_scales)
         nc.sync.dma_start(out=x_table[:].bitcast(I32), in_=words_of(x_words))
-        load_scale_rows(nc.scalar, x_scale_table, 0, x_scales)
-        two_list = load_list("two_list", two)
         gain = tile("gain", [P, PACK], F32)
-        nc.sync.dma_start(out=gain[:], in_=gn.rearrange("(p t) o -> p (t o)", t=PACK))
+        nc.gpsimd.dma_start(out=gain[:], in_=gn.rearrange("(p t) o -> p (t o)", t=PACK))
+        two_list = load_list("two_list", two)
         n1_list = load_list("n1_list", n1)
         n2_list = load_list("n2_list", n2)
-        w1_plain = tile("w1_plain", [P, N], U32)
-        w2_plain = tile("w2_plain", [P, N], U32)
-        nc.sync.dma_start(out=w2_plain[:].bitcast(I32), in_=words_of(w2_words))
-        nc.sync.dma_start(out=w1_plain[:].bitcast(I32), in_=words_of(w1_words))
-        load_scale_rows(nc.sync, w_plane_plain, 4, w2_scales)
-        load_scale_rows(nc.sync, w_plane_plain, 0, w1_scales)
         n4_list = load_list("n4_list", n4)
         n3_list = load_list("n3_list", n3)
 
         d_bytes = tile("d_bytes", [P, H], U8)
         nc.vector.tensor_copy(d_bytes[:], d_scale_table[:].indirect(k1_list[:]))
-        d_bytes_dealt = tile("d_bytes_dealt", [P, H], U8)
-        deal(d_bytes_dealt[:], d_bytes[:])
-        for j in range(4):
+        d_plane = tile("d_plane", [P, H], U8)
+        deal(d_plane[:], d_bytes[:])
+        for e in range(2):
             nc.scalar.dma_start(
-                out=d_plane[j:P:32, :].bitcast(I32), in_=d_bytes_dealt[8 * j : P : 32, :].bitcast(I32)
+                out=d_plane[2 + e : P : 32, :].bitcast(I32), in_=d_plane[16 + e : P : 32, :].bitcast(I32)
             )
-        x_plane = tile("x_plane", [P, S], U8)
-        nc.vector.tensor_copy(x_plane[:], x_scale_table[:].indirect(offs_list[:]))
         d_picked = tile("d_picked", [P, H], U32)
         nc.vector.tensor_copy(d_picked[:], d_table[:].indirect(k1_list[:]))
         d_codes = tile("d_codes", [P, H], U32)
         deal(d_codes[:], d_picked[:])
+        x_plane = tile("x_plane", [P, S], U8)
+        nc.vector.tensor_copy(x_plane[:], x_scale_table[:].indirect(offs_list[:]))
+
+        w_plain = tile("w_plain", [P, 2, N], U32, tag="d_table")
+        nc.sync.dma_start(out=w_plain[:, 1, :].bitcast(I32), in_=words_of(w2_words))
+        nc.sync.dma_start(out=w_plain[:, 0, :].bitcast(I32), in_=words_of(w1_words))
+        w_plane_plain = tile("w_plane_plain", [P, N], U8, tag="d_picked")
+        nc.gpsimd.memset(w_plane_plain[:].bitcast(I32), 0)
+        load_scale_rows(nc.sync, w_plane_plain, 4, w2_scales)
+        load_scale_rows(nc.sync, w_plane_plain, 0, w1_scales)
 
         scaled_gain = tile("scaled_gain", [P, PACK], F32)
-        nc.gpsimd.tensor_scalar(scaled_gain[:], gain[:], 0.0625, 0.0, ALU.mult, ALU.add)
+        nc.scalar.activation(scaled_gain[:], gain[:], COPY, scale=0.0625)
+        minus_gain = tile("minus_gain", [P, 1], F32)
+        nc.scalar.activation(minus_gain[:], gain[:, FUSED : FUSED + 1], COPY, scale=-0.0625)
+        minus_h = tile("minus_h", [P, S], F32)
 
         h_rows = [tile("h_rows%d" % t, [P, S], F32) for t in range(PACK)]
+        x_codes = []
         for c, (lo, hi) in enumerate(CHUNKS):
-            x_codes = tile("x_codes%d" % c, [P, hi - lo], U32)
-            nc.vector.tensor_copy(x_codes[:], x_table[:].indirect(offs_list[:, lo // 16 : hi // 16]))
-            for t in range(PACK):
-                cols = slice(P * t, P * (t + 1))
-                bank = psum.tile([P, hi - lo], F32, name="h_bank%d_%d" % (c, t), tag="bank%d" % (PACK * c + t))
+            x_codes.append(tile("x_codes%d" % c, [P, hi - lo], U32))
+            nc.vector.tensor_copy(x_codes[c][:], x_table[:].indirect(offs_list[:, lo // 16 : hi // 16]))
+        h_banks = {}
+        for t in range(PACK):
+            cols = slice(P * t, P * (t + 1))
+            for c, (lo, hi) in enumerate(CHUNKS):
+                h_banks[c, t] = psum.tile([P, hi - lo], F32, name="h_bank%d_%d" % (c, t), tag="bank%d" % (PACK * c + t))
                 nc.tensor.matmul_mx(
-                    out=bank[:], lhsT=d_codes[:, cols].bitcast(FP8X4), lhsT_scale=d_plane[:, cols],
-                    rhs=x_codes[:].bitcast(FP8X4), rhs_scale=x_plane[:, lo:hi], start=True, stop=True,
+                    out=h_banks[c, t][:], lhsT=d_codes[:, cols].bitcast(FP8X4), lhsT_scale=d_plane[:, cols],
+                    rhs=x_codes[c][:].bitcast(FP8X4), rhs_scale=x_plane[:, lo:hi], start=True, stop=True,
                 )
-                nc.scalar.activation(h_rows[t][:, lo:hi], bank[:], COPY, scale=scaled_gain[:, t : t + 1])
 
         two_codes = tile("two_codes", [P, S], U32)
-        nc.vector.tensor_copy(two_codes[:], x_table[:].indirect(two_list[:]))
         two_plane = tile("two_plane", [P, S], U8)
         nc.vector.tensor_copy(two_plane[:], x_scale_table[:].indirect(two_list[:]))
+        nc.vector.tensor_copy(two_codes[:], x_table[:].indirect(two_list[:]))
         w1_codes = tile("w1_codes", [P, N], U32)
         w2_codes = tile("w2_codes", [P, N], U32)
         w_plane = tile("w_plane", [P, N], U8)
-        deal(w2_codes[:], w2_plain[:])
-        deal(w_plane[:], w_plane_plain[:])
-        deal(w1_codes[:], w1_plain[:])
 
+        widths = [hi - lo for lo, hi in CHUNKS]
+        at_n1 = [tile("at_n1_%d" % c, [P, PACK - 1, n], F32) for c, n in enumerate(widths)]
+        at_n2 = [tile("at_n2_%d" % c, [P, PACK - 1, n], F32) for c, n in enumerate(widths)]
+        pa = [tile("pa%d" % c, [P, PACK, n], F32) for c, n in enumerate(widths)]
+        pb = [tile("pb%d" % c, [P, PACK, n], F32) for c, n in enumerate(widths)]
+        capped = [tile("capped%d" % c, [P, PACK, n], F32) for c, n in enumerate(widths)]
+        z_pairs = [tile("z_pairs%d" % c, [P, 2, n, 2], BF16) for c, n in enumerate(widths)]
+        z_grouped = [tile("z_grouped%d" % c, [P, n * PACK], BF16) for c, n in enumerate(widths)]
+        z_codes = [tile("z_codes%d" % c, [P, n], U32) for c, n in enumerate(widths)]
+        z_plane = [tile("z_plane%d" % c, [P, n], U8) for c, n in enumerate(widths)]
         h2_rows = [tile("h2_rows%d" % t, [P, S], F32) for t in range(PACK)]
-        h2_banks = []
-        for c, (lo, hi) in enumerate(CHUNKS):
-            n = hi - lo
+        h2_banks = {}
+
+        def h_out(c, t):
+            lo, hi = CHUNKS[c]
+            nc.scalar.activation(h_rows[t][:, lo:hi], h_banks[c, t][:], COPY, scale=scaled_gain[:, t : t + 1])
+            if t == FUSED:
+                nc.scalar.activation(minus_h[:, lo:hi], h_banks[c, t][:], COPY, scale=minus_gain[:])
+
+        def neighbours(c, t):
+            lo, hi = CHUNKS[c]
             picks = slice(lo // 16, hi // 16)
-            at_n1 = tile("at_n1_%d" % c, [P, PACK, n], F32)
-            at_n2 = tile("at_n2_%d" % c, [P, PACK, n], F32)
-            pa = tile("pa%d" % c, [P, PACK, n], F32)
-            pb = tile("pb%d" % c, [P, PACK, n], F32)
-            for t in range(PACK):
-                nc.scalar.activation(at_n1[:, t, :], h_rows[t][:].indirect(n1_list[:, picks]), COPY)
-                nc.scalar.activation(at_n2[:, t, :], h_rows[t][:].indirect(n2_list[:, picks]), COPY)
-                nc.vector.tensor_tensor(pa[:, t, :], h_rows[t][:, lo:hi], at_n1[:, t, :], ALU.subtract)
-                nc.vector.tensor_tensor(pb[:, t, :], at_n2[:, t, :], h_rows[t][:, lo:hi], ALU.subtract)
-            capped = tile("capped%d" % c, [P, PACK, n], F32)
-            z_pairs = tile("z_pairs%d" % c, [P, 2, n, 2], BF16)
-            for u in range(2):
-                pair = slice(2 * u, 2 * u + 2)
-                nc.vector.scalar_tensor_tensor(
-                    capped[:, pair, :], pb[:, pair, :], 0.0, pa[:, pair, :], ALU.max, ALU.min
-                )
-                nc.vector.scalar_tensor_tensor(
-                    z_pairs[:, u, :, :], pb[:, pair, :].rearrange("p e j -> p j e"), 0.0,
-                    capped[:, pair, :].rearrange("p e j -> p j e"), ALU.min, ALU.max,
-                )
-            z_grouped = tile("z_grouped%d" % c, [P, n * PACK], BF16)
-            nc.vector.tensor_copy(
-                out=z_grouped[:].bitcast(F32).rearrange("p (j u) -> p j u", u=2),
-                in_=z_pairs[:].rearrange("p u j e -> p (u j e)").bitcast(F32).rearrange("p (u j) -> p j u", u=2),
+            nc.scalar.activation(at_n1[c][:, t - 1, :], h_rows[t][:].indirect(n1_list[:, picks]), COPY)
+            nc.scalar.activation(at_n2[c][:, t - 1, :], h_rows[t][:].indirect(n2_list[:, picks]), COPY)
+
+        def differences(c, t):
+            lo, hi = CHUNKS[c]
+            picks = slice(lo // 16, hi // 16)
+            if t == FUSED:
+                nc.vector.tensor_tensor(pa[c][:, t, :], minus_h[:].indirect(n1_list[:, picks]), h_rows[t][:, lo:hi], ALU.add)
+                nc.vector.tensor_tensor(pb[c][:, t, :], h_rows[t][:].indirect(n2_list[:, picks]), minus_h[:, lo:hi], ALU.add)
+            else:
+                nc.vector.tensor_tensor(pa[c][:, t, :], h_rows[t][:, lo:hi], at_n1[c][:, t - 1, :], ALU.subtract)
+                nc.vector.tensor_tensor(pb[c][:, t, :], at_n2[c][:, t - 1, :], h_rows[t][:, lo:hi], ALU.subtract)
+
+        def cap(c, u):
+            pair = slice(2 * u, 2 * u + 2)
+            nc.vector.scalar_tensor_tensor(capped[c][:, pair, :], pb[c][:, pair, :], 0.0, pa[c][:, pair, :], ALU.max, ALU.min)
+
+        def minmod(c, u):
+            pair = slice(2 * u, 2 * u + 2)
+            nc.vector.scalar_tensor_tensor(
+                z_pairs[c][:, u, :, :], pb[c][:, pair, :].rearrange("p e j -> p j e"), 0.0,
+                capped[c][:, pair, :].rearrange("p e j -> p j e"), ALU.min, ALU.max,
             )
-            z_codes = tile("z_codes%d" % c, [P, n], U32)
-            z_plane = tile("z_plane%d" % c, [P, n], U8)
-            nc.vector.quantize_mx(out=z_codes[:].bitcast(FP8X4), scales=z_plane[:], in_=z_grouped[:])
-            banks = []
+
+        def weave(grouped, pairs):
+            nc.vector.tensor_copy(
+                out=grouped.bitcast(F32).rearrange("p (j u) -> p j u", u=2),
+                in_=pairs[:].rearrange("p u j e -> p (u j e)").bitcast(F32).rearrange("p (u j) -> p j u", u=2),
+            )
+
+        def open_sums(c):
+            lo, hi = CHUNKS[c]
             for t in range(PACK):
                 cols = slice(P * t, P * (t + 1))
-                bank = psum.tile([P, n], F32, name="h2_bank%d_%d" % (c, t), tag="bank%d" % (PACK * c + t))
+                bank = psum.tile([P, hi - lo], F32, name="h2_bank%d_%d" % (c, t), tag="bank%d" % (PACK * c + t))
                 nc.tensor.matmul_mx(
                     out=bank[:], lhsT=w2_codes[:, cols].bitcast(FP8X4), lhsT_scale=w_plane[4:P, cols],
                     rhs=two_codes[:, lo:hi].bitcast(FP8X4), rhs_scale=two_plane[:, lo:hi], start=True, stop=False,
                 )
-                banks.append(bank)
+                h2_banks[c, t] = bank
+
+        def close_sums(c):
+            nc.vector.quantize_mx(out=z_codes[c][:].bitcast(FP8X4), scales=z_plane[c][:], in_=z_grouped[c][:])
             for t in (0, 1, 3, 2):
                 cols = slice(P * t, P * (t + 1))
                 nc.tensor.matmul_mx(
-                    out=banks[t][:], lhsT=w1_codes[:, cols].bitcast(FP8X4), lhsT_scale=w_plane[:, cols],
-                    rhs=z_codes[:].bitcast(FP8X4), rhs_scale=z_plane[:], start=False, stop=True,
+                    out=h2_banks[c, t][:], lhsT=w1_codes[:, cols].bitcast(FP8X4), lhsT_scale=w_plane[:, cols],
+                    rhs=z_codes[c][:].bitcast(FP8X4), rhs_scale=z_plane[c][:], start=False, stop=True,
                 )
-            h2_banks.append(banks)
+
+        for t in range(PACK):
+            h_out(0, t)
+            h_out(1, t)
+            if t != FUSED:
+                neighbours(0, t)
+            if t == 1:
+                neighbours(1, t)
+        neighbours(1, 2)
+        neighbours(1, 3)
+
+        differences(0, 0)
+        differences(1, 0)
+        differences(0, 1)
+        deal(w2_codes[:], w_plain[:, 1, :])
+        cap(0, 0)
+        differences(1, 1)
+        minmod(0, 0)
+        deal(w_plane[:], w_plane_plain[:])
+        open_sums(0)
+        open_sums(1)
+        cap(1, 0)
+        differences(0, 2)
+        minmod(1, 0)
+        deal(w1_codes[:], w_plain[:, 0, :])
+        differences(0, 3)
+        cap(0, 1)
+        differences(1, 2)
+        minmod(0, 1)
+        differences(1, 3)
+        weave(z_grouped[0][:], z_pairs[0])
+        cap(1, 1)
+        close_sums(0)
+        minmod(1, 1)
+        weave(z_grouped[1][:], z_pairs[1])
+        close_sums(1)
 
         def leave_psum(c, t):
             lo, hi = CHUNKS[c]
-            nc.scalar.copy(h2_rows[t][:, lo:hi], h2_banks[c][t][:])
+            nc.scalar.copy(h2_rows[t][:, lo:hi], h2_banks[c, t][:])
 
         def leave_psum_vector(c, t):
             lo, hi = CHUNKS[c]
-            nc.vector.tensor_copy(h2_rows[t][:, lo:hi], h2_banks[c][t][:])
+            nc.vector.tensor_copy(h2_rows[t][:, lo:hi], h2_banks[c, t][:])
 
         old = [tile("old%d" % t, [P, W], F32) for t in range(PACK)]
         pull = [tile("pull%d" % t, [P, W], F32) for t in range(PACK)]
-        out_pairs = tile("out_pairs", [P, 2, S, 2], BF16)
+        left_pairs = tile("left_pairs", [P, 2, SPLIT, 2], BF16)
+        right_pairs = tile("right_pairs", [P, 2, S - SPLIT, 2], BF16)
         out_rows = out_0.rearrange("(p t) j -> p t j", t=PACK)
 
         def fetch_pull(t):
@@ -209,7 +271,10 @@ def tile_picked_pqmixminmodkdif_none_po_kernel(
             nc.sync.dma_start(out=out_rows[:, t, :], in_=h2_rows[t][:])
 
         def round_rows(t):
-            nc.vector.tensor_copy(out=out_pairs[:, t // 2, :, t % 2], in_=h2_rows[t][:])
+            nc.vector.tensor_copy(out=left_pairs[:, t // 2, :, t % 2], in_=h2_rows[t][:, :SPLIT])
+
+        def round_right(t):
+            nc.scalar.copy(out=right_pairs[:, t // 2, :, t % 2], in_=h2_rows[t][:, SPLIT:])
 
         last = len(CHUNKS) - 1
         for c in range(last):
@@ -217,33 +282,40 @@ def tile_picked_pqmixminmodkdif_none_po_kernel(
                 leave_psum(c, t)
         leave_psum(last, 0)
         leave_psum_vector(last, 1)
+        fetch_pull(0)
         nc.vector.tensor_copy(old[0][:], h2_rows[0][:].indirect(n3_list[:]))
         fetch_pull(1)
-        fetch_pull(0)
-        fetch_sum(1)
         scatter_sum(0)
+        fetch_sum(1)
         leave_psum(last, 3)
-        fetch_pull(3)
         leave_psum(last, 2)
+        fetch_pull(3)
+        fetch_pull(2)
         scatter_copy(1)
         fetch_sum(3)
+        fetch_sum(2)
         round_rows(0)
-        fetch_pull(2)
-        nc.vector.tensor_copy(old[2][:], h2_rows[2][:].indirect(n3_list[:]))
+        round_rows(1)
+        round_right(0)
+        round_right(1)
         scatter_copy(3)
-        scatter_sum(2)
-        for t in (1, 2, 3):
-            round_rows(t)
+        nc.vector.tensor_copy(h2_rows[2][:].indirect(n3_list[:]), old[2][:])
+        nc.sync.dma_start(out=out_rows[:, 2, :], in_=h2_rows[2][:])
+        round_right(3)
+        round_rows(3)
+        round_rows(2)
+        round_right(2)
 
         out_grouped = tile("out_grouped", [P, S * PACK], BF16)
-        nc.vector.tensor_copy(
-            out=out_grouped[:].bitcast(F32).rearrange("p (j u) -> p j u", u=2),
-            in_=out_pairs[:].rearrange("p u j e -> p (u j e)").bitcast(F32).rearrange("p (u j) -> p j u", u=2),
-        )
+        weave(out_grouped[:, : SPLIT * PACK], left_pairs)
+        weave(out_grouped[:, SPLIT * PACK :], right_pairs)
         out_codes = tile("out_codes", [P, S], U32)
         out_plane = tile("out_plane", [P, S], U8)
-        nc.vector.quantize_mx(out=out_codes[:].bitcast(FP8X4), scales=out_plane[:], in_=out_grouped[:])
-        nc.sync.dma_start(out=words_of(out_1), in_=out_codes[:].bitcast(I32))
+        for lo, hi in ((0, SPLIT), (SPLIT, S)):
+            nc.vector.quantize_mx(
+                out=out_codes[:, lo:hi].bitcast(FP8X4), scales=out_plane[:, lo:hi], in_=out_grouped[:, PACK * lo : PACK * hi]
+            )
+            nc.sync.dma_start(out=words_of(out_1)[:, lo:hi], in_=out_codes[:, lo:hi].bitcast(I32))
         for q in range(4):
             queue = nc.scalar if q % 2 == 0 else nc.sync
             queue.dma_start(

@@ -12,13 +12,17 @@ FP8X4 = mybir.dt.float8_e4m3fn_x4
 ALU = mybir.AluOpType
 COPY = mybir.ActivationFunctionType.Copy
 
-K, T, S, N, G, H, W = 512, 1024, 512, 512, 2048, 512, 384
+T, G = 1024, 2048
+S, H, N, W = 512, 512, 512, 384
 P = 128
 PACK = 4
+QUADRANTS = 4
+PER_COLUMN = 16
 FLOPS = 3 * 2 * 512 * 512 * 512
-CHUNKS = ((0, 256), (256, 512))
-FUSED = 0
-SPLIT = 384
+
+HALF = S // 2
+HALVES = (slice(0, HALF), slice(HALF, S))
+LEFT = 384
 
 
 def tile_picked_pqmixminmodkdif_none_po_kernel(
@@ -26,9 +30,6 @@ def tile_picked_pqmixminmodkdif_none_po_kernel(
     offs, k1, n1, n2, two, n3, n4, out_0, out_1, out_2,
 ):
     nc = tc.nc
-
-    def words_of(dram):
-        return dram[0].rearrange("p n t -> p (n t)").bitcast(I32)
 
     with ExitStack() as ctx:
         lists = ctx.enter_context(tc.tile_pool(name="lists", bufs=1))
@@ -38,15 +39,24 @@ def tile_picked_pqmixminmodkdif_none_po_kernel(
         def tile(name, shape, dtype, tag=None):
             return keep.tile(shape, dtype, name=name, tag=tag or name, align_bytes=64)
 
+        def bank(name, half, t):
+            return psum.tile([P, HALF], F32, name=name, tag="bank%d" % (PACK * half + t))
+
+        def words_of(dram):
+            return dram[0].rearrange("p c t -> p (c t)").bitcast(I32)
+
         def load_list(name, dram):
             held = lists.tile(list(dram.shape), U16, name=name)
             nc.sync.dma_start(held[:], dram)
             return held
 
-        def load_scale_rows(queue, plane, first_row, dram):
-            for q in range(4):
-                queue.dma_start(
-                    out=plane[32 * q + first_row : 32 * q + first_row + 4, :].bitcast(I32),
+        def entries(held, cols):
+            return held[:, cols.start // PER_COLUMN : cols.stop // PER_COLUMN]
+
+        def load_plane(plane, first, dram):
+            for q in range(QUADRANTS):
+                nc.sync.dma_start(
+                    out=plane[32 * q + first : 32 * q + first + 4, :].bitcast(I32),
                     in_=dram[0, 4 * q : 4 * q + 4, :].bitcast(I32),
                 )
 
@@ -54,6 +64,25 @@ def tile_picked_pqmixminmodkdif_none_po_kernel(
             nc.vector.tensor_copy(
                 out=dealt.rearrange("p (t m) -> p m t", t=PACK),
                 in_=plain.rearrange("p (m t) -> p m t", t=PACK),
+            )
+
+        def weave(grouped, pairs, cols):
+            nc.vector.tensor_copy(
+                out=grouped.bitcast(F32).rearrange("p (c u) -> p c u", u=2)[:, cols, :],
+                in_=pairs[:].rearrange("p u c e -> p (u c e)").bitcast(F32).rearrange("p (u c) -> p c u", u=2)[:, cols, :],
+            )
+
+        def quantise(codes, plane, grouped, cols):
+            nc.vector.quantize_mx(
+                out=codes[:, cols].bitcast(FP8X4), scales=plane[:, cols],
+                in_=grouped[:, PACK * cols.start : PACK * cols.stop],
+            )
+
+        def multiply(out, t, lhs_codes, lhs_plane, rhs_codes, rhs_plane, start, stop):
+            rows = slice(P * t, P * (t + 1))
+            nc.tensor.matmul_mx(
+                out=out, lhsT=lhs_codes[:, rows].bitcast(FP8X4), lhsT_scale=lhs_plane[:, rows],
+                rhs=rhs_codes.bitcast(FP8X4), rhs_scale=rhs_plane, start=start, stop=stop,
             )
 
         d_scale_table = tile("d_scale_table", [P, G], U8)
@@ -68,7 +97,7 @@ def tile_picked_pqmixminmodkdif_none_po_kernel(
         d_table = tile("d_table", [P, G], U32)
         x_table = tile("x_table", [P, T], U32)
         nc.sync.dma_start(out=d_table[:].bitcast(I32), in_=words_of(d_words))
-        load_scale_rows(nc.sync, x_scale_table, 0, x_scales)
+        load_plane(x_scale_table, 0, x_scales)
         nc.sync.dma_start(out=x_table[:].bitcast(I32), in_=words_of(x_words))
         gain = tile("gain", [P, PACK], F32)
         nc.gpsimd.dma_start(out=gain[:], in_=gn.rearrange("(p t) o -> p (t o)", t=PACK))
@@ -98,225 +127,222 @@ def tile_picked_pqmixminmodkdif_none_po_kernel(
         nc.sync.dma_start(out=w_plain[:, 0, :].bitcast(I32), in_=words_of(w1_words))
         w_plane_plain = tile("w_plane_plain", [P, N], U8, tag="d_picked")
         nc.gpsimd.memset(w_plane_plain[:].bitcast(I32), 0)
-        load_scale_rows(nc.sync, w_plane_plain, 4, w2_scales)
-        load_scale_rows(nc.sync, w_plane_plain, 0, w1_scales)
+        load_plane(w_plane_plain, 4, w2_scales)
+        load_plane(w_plane_plain, 0, w1_scales)
 
         scaled_gain = tile("scaled_gain", [P, PACK], F32)
         nc.scalar.activation(scaled_gain[:], gain[:], COPY, scale=0.0625)
         minus_gain = tile("minus_gain", [P, 1], F32)
-        nc.scalar.activation(minus_gain[:], gain[:, FUSED : FUSED + 1], COPY, scale=-0.0625)
+        nc.scalar.activation(minus_gain[:], gain[:, 0:1], COPY, scale=-0.0625)
         minus_h = tile("minus_h", [P, S], F32)
-
         h_rows = [tile("h_rows%d" % t, [P, S], F32) for t in range(PACK)]
-        x_codes = []
-        for c, (lo, hi) in enumerate(CHUNKS):
-            x_codes.append(tile("x_codes%d" % c, [P, hi - lo], U32))
-            nc.vector.tensor_copy(x_codes[c][:], x_table[:].indirect(offs_list[:, lo // 16 : hi // 16]))
+        x_codes = [tile("x_codes%d" % half, [P, HALF], U32) for half in range(2)]
+        for half, cols in enumerate(HALVES):
+            nc.vector.tensor_copy(x_codes[half][:], x_table[:].indirect(entries(offs_list, cols)))
         h_banks = {}
         for t in range(PACK):
-            cols = slice(P * t, P * (t + 1))
-            for c, (lo, hi) in enumerate(CHUNKS):
-                h_banks[c, t] = psum.tile([P, hi - lo], F32, name="h_bank%d_%d" % (c, t), tag="bank%d" % (PACK * c + t))
-                nc.tensor.matmul_mx(
-                    out=h_banks[c, t][:], lhsT=d_codes[:, cols].bitcast(FP8X4), lhsT_scale=d_plane[:, cols],
-                    rhs=x_codes[c][:].bitcast(FP8X4), rhs_scale=x_plane[:, lo:hi], start=True, stop=True,
-                )
+            for half, cols in enumerate(HALVES):
+                h_banks[half, t] = bank("h_bank%d_%d" % (half, t), half, t)
+                multiply(h_banks[half, t][:], t, d_codes, d_plane, x_codes[half][:], x_plane[:, cols], True, True)
 
         two_codes = tile("two_codes", [P, S], U32)
         two_plane = tile("two_plane", [P, S], U8)
         nc.vector.tensor_copy(two_plane[:], x_scale_table[:].indirect(two_list[:]))
         nc.vector.tensor_copy(two_codes[:], x_table[:].indirect(two_list[:]))
+
         w1_codes = tile("w1_codes", [P, N], U32)
         w2_codes = tile("w2_codes", [P, N], U32)
         w_plane = tile("w_plane", [P, N], U8)
-
-        widths = [hi - lo for lo, hi in CHUNKS]
-        at_n1 = [tile("at_n1_%d" % c, [P, PACK - 1, n], F32) for c, n in enumerate(widths)]
-        at_n2 = [tile("at_n2_%d" % c, [P, PACK - 1, n], F32) for c, n in enumerate(widths)]
-        pa = [tile("pa%d" % c, [P, PACK, n], F32) for c, n in enumerate(widths)]
-        pb = [tile("pb%d" % c, [P, PACK, n], F32) for c, n in enumerate(widths)]
-        capped = [tile("capped%d" % c, [P, PACK, n], F32) for c, n in enumerate(widths)]
-        z_pairs = [tile("z_pairs%d" % c, [P, 2, n, 2], BF16) for c, n in enumerate(widths)]
-        z_grouped = [tile("z_grouped%d" % c, [P, n * PACK], BF16) for c, n in enumerate(widths)]
-        z_codes = [tile("z_codes%d" % c, [P, n], U32) for c, n in enumerate(widths)]
-        z_plane = [tile("z_plane%d" % c, [P, n], U8) for c, n in enumerate(widths)]
-        h2_rows = [tile("h2_rows%d" % t, [P, S], F32) for t in range(PACK)]
+        at_n1, at_n2 = {}, {}
+        pa = [tile("pa%d" % half, [P, PACK, HALF], F32) for half in range(2)]
+        pb = [tile("pb%d" % half, [P, PACK, HALF], F32) for half in range(2)]
+        capped = [tile("capped%d" % half, [P, PACK, HALF], F32) for half in range(2)]
+        z_pairs = [tile("z_pairs%d" % half, [P, 2, HALF, 2], BF16) for half in range(2)]
+        z_grouped = [tile("z_grouped%d" % half, [P, HALF * PACK], BF16) for half in range(2)]
+        z_codes = [tile("z_codes%d" % half, [P, HALF], U32) for half in range(2)]
+        z_plane = [tile("z_plane%d" % half, [P, HALF], U8) for half in range(2)]
         h2_banks = {}
 
-        def h_out(c, t):
-            lo, hi = CHUNKS[c]
-            nc.scalar.activation(h_rows[t][:, lo:hi], h_banks[c, t][:], COPY, scale=scaled_gain[:, t : t + 1])
-            if t == FUSED:
-                nc.scalar.activation(minus_h[:, lo:hi], h_banks[c, t][:], COPY, scale=minus_gain[:])
+        def empty_h(t):
+            for half, cols in enumerate(HALVES):
+                nc.scalar.activation(h_rows[t][:, cols], h_banks[half, t][:], COPY, scale=scaled_gain[:, t : t + 1])
+                if t == 0:
+                    nc.scalar.activation(minus_h[:, cols], h_banks[half, t][:], COPY, scale=minus_gain[:])
 
-        def neighbours(c, t):
-            lo, hi = CHUNKS[c]
-            picks = slice(lo // 16, hi // 16)
-            nc.scalar.activation(at_n1[c][:, t - 1, :], h_rows[t][:].indirect(n1_list[:, picks]), COPY)
-            nc.scalar.activation(at_n2[c][:, t - 1, :], h_rows[t][:].indirect(n2_list[:, picks]), COPY)
+        def fetch_n1(half, t):
+            at_n1[half, t] = tile("at_n1_%d_%d" % (half, t), [P, HALF], F32)
+            nc.scalar.activation(at_n1[half, t][:], h_rows[t][:].indirect(entries(n1_list, HALVES[half])), COPY)
 
-        def differences(c, t):
-            lo, hi = CHUNKS[c]
-            picks = slice(lo // 16, hi // 16)
-            if t == FUSED:
-                nc.vector.tensor_tensor(pa[c][:, t, :], minus_h[:].indirect(n1_list[:, picks]), h_rows[t][:, lo:hi], ALU.add)
-                nc.vector.tensor_tensor(pb[c][:, t, :], h_rows[t][:].indirect(n2_list[:, picks]), minus_h[:, lo:hi], ALU.add)
+        def fetch_n2(half, t):
+            at_n2[half, t] = tile("at_n2_%d_%d" % (half, t), [P, HALF], F32)
+            nc.scalar.activation(at_n2[half, t][:], h_rows[t][:].indirect(entries(n2_list, HALVES[half])), COPY)
+
+        def fetch_both(half, t):
+            fetch_n1(half, t)
+            fetch_n2(half, t)
+
+        def make_pa(half, t):
+            own = h_rows[t][:, HALVES[half]]
+            if (half, t) in at_n1:
+                nc.vector.tensor_tensor(pa[half][:, t, :], own, at_n1[half, t][:], ALU.subtract)
             else:
-                nc.vector.tensor_tensor(pa[c][:, t, :], h_rows[t][:, lo:hi], at_n1[c][:, t - 1, :], ALU.subtract)
-                nc.vector.tensor_tensor(pb[c][:, t, :], at_n2[c][:, t - 1, :], h_rows[t][:, lo:hi], ALU.subtract)
+                nc.vector.tensor_tensor(pa[half][:, t, :], minus_h[:].indirect(entries(n1_list, HALVES[half])), own, ALU.add)
 
-        def cap(c, u):
-            pair = slice(2 * u, 2 * u + 2)
-            nc.vector.scalar_tensor_tensor(capped[c][:, pair, :], pb[c][:, pair, :], 0.0, pa[c][:, pair, :], ALU.max, ALU.min)
+        def make_pb(half, t):
+            cols = HALVES[half]
+            if (half, t) in at_n2:
+                nc.vector.tensor_tensor(pb[half][:, t, :], at_n2[half, t][:], h_rows[t][:, cols], ALU.subtract)
+            else:
+                nc.vector.tensor_tensor(pb[half][:, t, :], h_rows[t][:].indirect(entries(n2_list, cols)), minus_h[:, cols], ALU.add)
 
-        def minmod(c, u):
+        def differences(half, t):
+            make_pa(half, t)
+            make_pb(half, t)
+
+        def cap(half, u, cols):
             pair = slice(2 * u, 2 * u + 2)
             nc.vector.scalar_tensor_tensor(
-                z_pairs[c][:, u, :, :], pb[c][:, pair, :].rearrange("p e j -> p j e"), 0.0,
-                capped[c][:, pair, :].rearrange("p e j -> p j e"), ALU.min, ALU.max,
+                capped[half][:, pair, cols], pb[half][:, pair, cols], 0.0, pa[half][:, pair, cols], ALU.max, ALU.min
             )
 
-        def weave(grouped, pairs):
-            nc.vector.tensor_copy(
-                out=grouped.bitcast(F32).rearrange("p (j u) -> p j u", u=2),
-                in_=pairs[:].rearrange("p u j e -> p (u j e)").bitcast(F32).rearrange("p (u j) -> p j u", u=2),
+        def minmod(half, u, cols):
+            pair = slice(2 * u, 2 * u + 2)
+            nc.vector.scalar_tensor_tensor(
+                z_pairs[half][:, u, cols, :], pb[half][:, pair, cols].rearrange("p e c -> p c e"), 0.0,
+                capped[half][:, pair, cols].rearrange("p e c -> p c e"), ALU.min, ALU.max,
             )
 
-        def open_sums(c):
-            lo, hi = CHUNKS[c]
+        def open_sums(half):
+            cols = HALVES[half]
             for t in range(PACK):
-                cols = slice(P * t, P * (t + 1))
-                bank = psum.tile([P, hi - lo], F32, name="h2_bank%d_%d" % (c, t), tag="bank%d" % (PACK * c + t))
-                nc.tensor.matmul_mx(
-                    out=bank[:], lhsT=w2_codes[:, cols].bitcast(FP8X4), lhsT_scale=w_plane[4:P, cols],
-                    rhs=two_codes[:, lo:hi].bitcast(FP8X4), rhs_scale=two_plane[:, lo:hi], start=True, stop=False,
-                )
-                h2_banks[c, t] = bank
+                h2_banks[half, t] = bank("h2_bank%d_%d" % (half, t), half, t)
+                multiply(h2_banks[half, t][:], t, w2_codes, w_plane[4:P, :], two_codes[:, cols], two_plane[:, cols], True, False)
 
-        def close_sums(c):
-            nc.vector.quantize_mx(out=z_codes[c][:].bitcast(FP8X4), scales=z_plane[c][:], in_=z_grouped[c][:])
-            for t in (0, 1, 3, 2):
-                cols = slice(P * t, P * (t + 1))
-                nc.tensor.matmul_mx(
-                    out=h2_banks[c, t][:], lhsT=w1_codes[:, cols].bitcast(FP8X4), lhsT_scale=w_plane[:, cols],
-                    rhs=z_codes[c][:].bitcast(FP8X4), rhs_scale=z_plane[c][:], start=False, stop=True,
-                )
+        def add_w1(half, t, cols):
+            multiply(
+                h2_banks[half, t][:, cols], t, w1_codes, w_plane, z_codes[half][:, cols], z_plane[half][:, cols],
+                False, cols.stop == HALF,
+            )
 
-        for t in range(PACK):
-            h_out(0, t)
-            h_out(1, t)
-            if t != FUSED:
-                neighbours(0, t)
-            if t == 1:
-                neighbours(1, t)
-        neighbours(1, 2)
-        neighbours(1, 3)
+        empty_h(0)
+        empty_h(1)
+        fetch_both(0, 1)
+        fetch_n2(1, 0)
+        fetch_both(1, 1)
+        empty_h(2)
+        empty_h(3)
+        for half in range(2):
+            fetch_both(half, 2)
+            fetch_both(half, 3)
 
+        whole = slice(0, HALF)
         differences(0, 0)
-        differences(1, 0)
         differences(0, 1)
-        deal(w2_codes[:], w_plain[:, 1, :])
-        cap(0, 0)
+        cap(0, 0, whole)
+        differences(1, 0)
+        minmod(0, 0, whole)
         differences(1, 1)
-        minmod(0, 0)
+        deal(w2_codes[:], w_plain[:, 1, :])
+        cap(1, 0, whole)
         deal(w_plane[:], w_plane_plain[:])
         open_sums(0)
         open_sums(1)
-        cap(1, 0)
-        differences(0, 2)
-        minmod(1, 0)
+        minmod(1, 0, whole)
         deal(w1_codes[:], w_plain[:, 0, :])
+        differences(0, 2)
         differences(0, 3)
-        cap(0, 1)
+        cap(0, 1, whole)
         differences(1, 2)
-        minmod(0, 1)
-        differences(1, 3)
-        weave(z_grouped[0][:], z_pairs[0])
-        cap(1, 1)
-        close_sums(0)
-        minmod(1, 1)
-        weave(z_grouped[1][:], z_pairs[1])
-        close_sums(1)
+        minmod(0, 1, whole)
+        make_pa(1, 3)
+        weave(z_grouped[0][:], z_pairs[0], whole)
+        make_pb(1, 3)
+        quantise(z_codes[0], z_plane[0], z_grouped[0], whole)
+        tile_order = (0, 1, 3, 2)
+        for t in tile_order:
+            add_w1(0, t, whole)
+        quarters = (slice(0, HALF // 2), slice(HALF // 2, HALF))
+        for cols in quarters:
+            cap(1, 1, cols)
+        for cols in quarters:
+            minmod(1, 1, cols)
+        for cols in quarters:
+            weave(z_grouped[1][:], z_pairs[1], cols)
+        for cols in quarters:
+            quantise(z_codes[1], z_plane[1], z_grouped[1], cols)
+        for tiles in (tile_order[:2], tile_order[2:]):
+            for cols in quarters:
+                for t in tiles:
+                    add_w1(1, t, cols)
 
-        def leave_psum(c, t):
-            lo, hi = CHUNKS[c]
-            nc.scalar.copy(h2_rows[t][:, lo:hi], h2_banks[c, t][:])
-
-        def leave_psum_vector(c, t):
-            lo, hi = CHUNKS[c]
-            nc.vector.tensor_copy(h2_rows[t][:, lo:hi], h2_banks[c, t][:])
-
-        old = [tile("old%d" % t, [P, W], F32) for t in range(PACK)]
+        h2_rows = [tile("h2_rows%d" % t, [P, S], F32) for t in range(PACK)]
         pull = [tile("pull%d" % t, [P, W], F32) for t in range(PACK)]
-        left_pairs = tile("left_pairs", [P, 2, SPLIT, 2], BF16)
-        right_pairs = tile("right_pairs", [P, 2, S - SPLIT, 2], BF16)
+        old = tile("old", [P, W], F32)
+        ra = {t: tile("ra%d" % t, [P, W], F32) for t in range(1, PACK)}
+        left_pairs = tile("left_pairs", [P, 2, LEFT, 2], BF16)
+        right_pairs = tile("right_pairs", [P, 2, S - LEFT, 2], BF16)
         out_rows = out_0.rearrange("(p t) j -> p t j", t=PACK)
+
+        def empty_h2(copy, half, t):
+            copy(h2_rows[t][:, HALVES[half]], h2_banks[half, t][:])
 
         def fetch_pull(t):
             nc.scalar.activation(pull[t][:], h2_rows[t][:].indirect(n4_list[:]), COPY, scale=-0.5)
 
-        def scatter_sum(t):
-            for lo in range(0, W, W // 2):
-                hi = lo + W // 2
-                nc.vector.tensor_tensor(
-                    h2_rows[t][:].indirect(n3_list[:, lo // 16 : hi // 16]), old[t][:, lo:hi], pull[t][:, lo:hi], ALU.add
-                )
+        def make_ra(t):
+            nc.vector.tensor_tensor(ra[t][:], h2_rows[t][:].indirect(n3_list[:]), pull[t][:], ALU.add)
+
+        def store_rows(t):
             nc.sync.dma_start(out=out_rows[:, t, :], in_=h2_rows[t][:])
 
-        def fetch_sum(t):
-            nc.vector.tensor_tensor(old[t][:], h2_rows[t][:].indirect(n3_list[:]), pull[t][:], ALU.add)
+        def scatter_on_scalar(t):
+            nc.scalar.activation(h2_rows[t][:].indirect(n3_list[:]), ra[t][:], COPY)
+            store_rows(t)
 
-        def scatter_copy(t):
-            nc.scalar.activation(h2_rows[t][:].indirect(n3_list[:]), old[t][:], COPY)
-            nc.sync.dma_start(out=out_rows[:, t, :], in_=h2_rows[t][:])
-
-        def round_rows(t):
-            nc.vector.tensor_copy(out=left_pairs[:, t // 2, :, t % 2], in_=h2_rows[t][:, :SPLIT])
+        def round_left(t):
+            nc.vector.tensor_copy(out=left_pairs[:, t // 2, :, t % 2], in_=h2_rows[t][:, :LEFT])
 
         def round_right(t):
-            nc.scalar.copy(out=right_pairs[:, t // 2, :, t % 2], in_=h2_rows[t][:, SPLIT:])
+            nc.scalar.copy(out=right_pairs[:, t // 2, :, t % 2], in_=h2_rows[t][:, LEFT:])
 
-        last = len(CHUNKS) - 1
-        for c in range(last):
-            for t in range(PACK):
-                leave_psum(c, t)
-        leave_psum(last, 0)
-        leave_psum_vector(last, 1)
+        for t in range(PACK):
+            empty_h2(nc.scalar.copy, 0, t)
+        empty_h2(nc.scalar.copy, 1, 0)
+        empty_h2(nc.vector.tensor_copy, 1, 1)
         fetch_pull(0)
-        nc.vector.tensor_copy(old[0][:], h2_rows[0][:].indirect(n3_list[:]))
+        nc.vector.tensor_copy(old[:], h2_rows[0][:].indirect(n3_list[:]))
         fetch_pull(1)
-        scatter_sum(0)
-        fetch_sum(1)
-        leave_psum(last, 3)
-        leave_psum(last, 2)
-        fetch_pull(3)
-        fetch_pull(2)
-        scatter_copy(1)
-        fetch_sum(3)
-        fetch_sum(2)
-        round_rows(0)
-        round_rows(1)
-        round_right(0)
-        round_right(1)
-        scatter_copy(3)
-        nc.vector.tensor_copy(h2_rows[2][:].indirect(n3_list[:]), old[2][:])
-        nc.sync.dma_start(out=out_rows[:, 2, :], in_=h2_rows[2][:])
+        for cols in (slice(0, W // 2), slice(W // 2, W)):
+            nc.vector.tensor_tensor(h2_rows[0][:].indirect(entries(n3_list, cols)), old[:, cols], pull[0][:, cols], ALU.add)
+        store_rows(0)
+        make_ra(1)
+        for t in tile_order[2:]:
+            empty_h2(nc.scalar.copy, 1, t)
+        for t in tile_order[2:]:
+            fetch_pull(t)
+        scatter_on_scalar(1)
+        for t in tile_order[2:]:
+            make_ra(t)
+        for round_part in (round_left, round_right):
+            round_part(0)
+            round_part(1)
+        scatter_on_scalar(3)
+        nc.vector.tensor_copy(h2_rows[2][:].indirect(n3_list[:]), ra[2][:])
+        store_rows(2)
         round_right(3)
-        round_rows(3)
-        round_rows(2)
+        round_left(3)
+        round_left(2)
         round_right(2)
 
         out_grouped = tile("out_grouped", [P, S * PACK], BF16)
-        weave(out_grouped[:, : SPLIT * PACK], left_pairs)
-        weave(out_grouped[:, SPLIT * PACK :], right_pairs)
+        weave(out_grouped[:, : LEFT * PACK], left_pairs, slice(0, LEFT))
+        weave(out_grouped[:, LEFT * PACK :], right_pairs, slice(0, S - LEFT))
         out_codes = tile("out_codes", [P, S], U32)
         out_plane = tile("out_plane", [P, S], U8)
-        for lo, hi in ((0, SPLIT), (SPLIT, S)):
-            nc.vector.quantize_mx(
-                out=out_codes[:, lo:hi].bitcast(FP8X4), scales=out_plane[:, lo:hi], in_=out_grouped[:, PACK * lo : PACK * hi]
-            )
-            nc.sync.dma_start(out=words_of(out_1)[:, lo:hi], in_=out_codes[:, lo:hi].bitcast(I32))
-        for q in range(4):
+        for cols in (slice(0, LEFT), slice(LEFT, S)):
+            quantise(out_codes, out_plane, out_grouped, cols)
+            nc.sync.dma_start(out=words_of(out_1)[:, cols], in_=out_codes[:, cols].bitcast(I32))
+        for q in range(QUADRANTS):
             queue = nc.scalar if q % 2 == 0 else nc.sync
             queue.dma_start(
                 out=out_2[0, 4 * q : 4 * q + 4, :].bitcast(I32), in_=out_plane[32 * q : 32 * q + 4, :].bitcast(I32)

@@ -279,7 +279,7 @@ def tile_picked_pqmixminmodkdif_none_po_kernel(
         pull = [tile("pull%d" % t, [P, W], F32) for t in range(PACK)]
         old = tile("old", [P, W], F32)
         ra = {t: tile("ra%d" % t, [P, W], F32) for t in range(1, PACK)}
-        left_pairs = tile("left_pairs", [P, 2, LEFT, 2], BF16)
+        left_pairs = tile("left_pairs", [P, 2, LEFT, 2], BF16, tag="pull2")
         right_pairs = tile("right_pairs", [P, 2, S - LEFT, 2], BF16)
         out_rows = out_0.rearrange("(p t) j -> p t j", t=PACK)
 
@@ -300,7 +300,7 @@ def tile_picked_pqmixminmodkdif_none_po_kernel(
             store_rows(t)
 
         def round_left(t):
-            nc.vector.tensor_copy(out=left_pairs[:, t // 2, :, t % 2], in_=h2_rows[t][:, :LEFT])
+            (nc.gpsimd if t < 2 else nc.vector).tensor_copy(out=left_pairs[:, t // 2, :, t % 2], in_=h2_rows[t][:, :LEFT])
 
         def round_right(t):
             nc.scalar.copy(out=right_pairs[:, t // 2, :, t % 2], in_=h2_rows[t][:, LEFT:])

from contextlib import ExitStack

import concourse.mybir as mybir

F32 = mybir.dt.float32
BF16 = mybir.dt.bfloat16
I32 = mybir.dt.int32
U32 = mybir.dt.uint32
U16 = mybir.dt.uint16
U8 = mybir.dt.uint8
FP8X4 = mybir.dt.float8_e4m3fn_x4
ALU = mybir.AluOpType
COPY = mybir.ActivationFunctionType.Copy

T, G = 1024, 2048
S, H, N, W = 512, 512, 512, 384
P = 128
PACK = 4
QUADRANTS = 4
PER_COLUMN = 16
FLOPS = 3 * 2 * 512 * 512 * 512

HALF = S // 2
HALVES = (slice(0, HALF), slice(HALF, S))
LEFT = 384


def tile_picked_pqmixminmodkdif_none_po_kernel(
    tc, x_words, x_scales, d_words, d_scales, gn, w1_words, w1_scales, w2_words, w2_scales,
    offs, k1, n1, n2, two, n3, n4, out_0, out_1, out_2,
):
    nc = tc.nc

    with ExitStack() as ctx:
        lists = ctx.enter_context(tc.tile_pool(name="lists", bufs=1))
        keep = ctx.enter_context(tc.tile_pool(name="keep", bufs=1))
        psum = ctx.enter_context(tc.psum_pool(name="psum", bufs=1))

        def tile(name, shape, dtype, tag=None):
            return keep.tile(shape, dtype, name=name, tag=tag or name, align_bytes=64)

        def bank(name, half, t):
            return psum.tile([P, HALF], F32, name=name, tag="bank%d" % (PACK * half + t))

        def words_of(dram):
            return dram[0].rearrange("p c t -> p (c t)").bitcast(I32)

        def load_list(name, dram):
            held = lists.tile(list(dram.shape), U16, name=name)
            nc.sync.dma_start(held[:], dram)
            return held

        def entries(held, cols):
            return held[:, cols.start // PER_COLUMN : cols.stop // PER_COLUMN]

        def load_plane(plane, first, dram):
            for q in range(QUADRANTS):
                nc.sync.dma_start(
                    out=plane[32 * q + first : 32 * q + first + 4, :].bitcast(I32),
                    in_=dram[0, 4 * q : 4 * q + 4, :].bitcast(I32),
                )

        def deal(dealt, plain):
            nc.vector.tensor_copy(
                out=dealt.rearrange("p (t m) -> p m t", t=PACK),
                in_=plain.rearrange("p (m t) -> p m t", t=PACK),
            )

        def weave(grouped, pairs, cols):
            nc.vector.tensor_copy(
                out=grouped.bitcast(F32).rearrange("p (c u) -> p c u", u=2)[:, cols, :],
                in_=pairs[:].rearrange("p u c e -> p (u c e)").bitcast(F32).rearrange("p (u c) -> p c u", u=2)[:, cols, :],
            )

        def quantise(codes, plane, grouped, cols):
            nc.vector.quantize_mx(
                out=codes[:, cols].bitcast(FP8X4), scales=plane[:, cols],
                in_=grouped[:, PACK * cols.start : PACK * cols.stop],
            )

        def multiply(out, t, lhs_codes, lhs_plane, rhs_codes, rhs_plane, start, stop):
            rows = slice(P * t, P * (t + 1))
            nc.tensor.matmul_mx(
                out=out, lhsT=lhs_codes[:, rows].bitcast(FP8X4), lhsT_scale=lhs_plane[:, rows],
                rhs=rhs_codes.bitcast(FP8X4), rhs_scale=rhs_plane, start=start, stop=stop,
            )

        d_scale_table = tile("d_scale_table", [P, G], U8)
        x_scale_table = tile("x_scale_table", [P, T], U8)
        nc.gpsimd.memset(d_scale_table[:].bitcast(I32), 0)
        nc.vector.memset(x_scale_table[:].bitcast(I32), 0)

        k1_list = load_list("k1_list", k1)
        offs_list = load_list("offs_list", offs)
        for e in range(2):
            nc.sync.dma_start(out=d_scale_table[e:P:16, :].bitcast(I32), in_=d_scales[0, e:16:2, :].bitcast(I32))
        d_table = tile("d_table", [P, G], U32)
        x_table = tile("x_table", [P, T], U32)
        nc.sync.dma_start(out=d_table[:].bitcast(I32), in_=words_of(d_words))
        load_plane(x_scale_table, 0, x_scales)
        nc.sync.dma_start(out=x_table[:].bitcast(I32), in_=words_of(x_words))
        gain = tile("gain", [P, PACK], F32)
        nc.gpsimd.dma_start(out=gain[:], in_=gn.rearrange("(p t) o -> p (t o)", t=PACK))
        two_list = load_list("two_list", two)
        n1_list = load_list("n1_list", n1)
        n2_list = load_list("n2_list", n2)
        n4_list = load_list("n4_list", n4)
        n3_list = load_list("n3_list", n3)

        d_bytes = tile("d_bytes", [P, H], U8)
        nc.vector.tensor_copy(d_bytes[:], d_scale_table[:].indirect(k1_list[:]))
        d_plane = tile("d_plane", [P, H], U8)
        deal(d_plane[:], d_bytes[:])
        for e in range(2):
            nc.scalar.dma_start(
                out=d_plane[2 + e : P : 32, :].bitcast(I32), in_=d_plane[16 + e : P : 32, :].bitcast(I32)
            )
        d_picked = tile("d_picked", [P, H], U32)
        nc.vector.tensor_copy(d_picked[:], d_table[:].indirect(k1_list[:]))
        d_codes = tile("d_codes", [P, H], U32)
        deal(d_codes[:], d_picked[:])
        x_plane = tile("x_plane", [P, S], U8)
        nc.vector.tensor_copy(x_plane[:], x_scale_table[:].indirect(offs_list[:]))

        w_plain = tile("w_plain", [P, 2, N], U32, tag="d_table")
        nc.sync.dma_start(out=w_plain[:, 1, :].bitcast(I32), in_=words_of(w2_words))
        nc.sync.dma_start(out=w_plain[:, 0, :].bitcast(I32), in_=words_of(w1_words))
        w_plane_plain = tile("w_plane_plain", [P, N], U8, tag="d_picked")
        nc.gpsimd.memset(w_plane_plain[:].bitcast(I32), 0)
        load_plane(w_plane_plain, 4, w2_scales)
        load_plane(w_plane_plain, 0, w1_scales)

        scaled_gain = tile("scaled_gain", [P, PACK], F32)
        nc.scalar.activation(scaled_gain[:], gain[:], COPY, scale=0.0625)
        minus_gain = tile("minus_gain", [P, 1], F32)
        nc.scalar.activation(minus_gain[:], gain[:, 0:1], COPY, scale=-0.0625)
        minus_h = tile("minus_h", [P, S], F32)
        h_rows = [tile("h_rows%d" % t, [P, S], F32) for t in range(PACK)]
        x_codes = [tile("x_codes%d" % half, [P, HALF], U32) for half in range(2)]
        for half, cols in enumerate(HALVES):
            nc.vector.tensor_copy(x_codes[half][:], x_table[:].indirect(entries(offs_list, cols)))
        h_banks = {}
        for t in range(PACK):
            for half, cols in enumerate(HALVES):
                h_banks[half, t] = bank("h_bank%d_%d" % (half, t), half, t)
                multiply(h_banks[half, t][:], t, d_codes, d_plane, x_codes[half][:], x_plane[:, cols], True, True)

        two_codes = tile("two_codes", [P, S], U32)
        two_plane = tile("two_plane", [P, S], U8)
        nc.vector.tensor_copy(two_plane[:], x_scale_table[:].indirect(two_list[:]))
        nc.vector.tensor_copy(two_codes[:], x_table[:].indirect(two_list[:]))

        w1_codes = tile("w1_codes", [P, N], U32)
        w2_codes = tile("w2_codes", [P, N], U32)
        w_plane = tile("w_plane", [P, N], U8)
        at_n1, at_n2 = {}, {}
        pa = [tile("pa%d" % half, [P, PACK, HALF], F32) for half in range(2)]
        pb = [tile("pb%d" % half, [P, PACK, HALF], F32) for half in range(2)]
        capped = [tile("capped%d" % half, [P, PACK, HALF], F32) for half in range(2)]
        z_pairs = [tile("z_pairs%d" % half, [P, 2, HALF, 2], BF16) for half in range(2)]
        z_grouped = [tile("z_grouped%d" % half, [P, HALF * PACK], BF16) for half in range(2)]
        z_codes = [tile("z_codes%d" % half, [P, HALF], U32) for half in range(2)]
        z_plane = [tile("z_plane%d" % half, [P, HALF], U8) for half in range(2)]
        h2_banks = {}

        def empty_h(t):
            for half, cols in enumerate(HALVES):
                nc.scalar.activation(h_rows[t][:, cols], h_banks[half, t][:], COPY, scale=scaled_gain[:, t : t + 1])
                if t == 0:
                    nc.scalar.activation(minus_h[:, cols], h_banks[half, t][:], COPY, scale=minus_gain[:])

        def fetch_n1(half, t):
            at_n1[half, t] = tile("at_n1_%d_%d" % (half, t), [P, HALF], F32)
            nc.scalar.activation(at_n1[half, t][:], h_rows[t][:].indirect(entries(n1_list, HALVES[half])), COPY)

        def fetch_n2(half, t):
            at_n2[half, t] = tile("at_n2_%d_%d" % (half, t), [P, HALF], F32)
            nc.scalar.activation(at_n2[half, t][:], h_rows[t][:].indirect(entries(n2_list, HALVES[half])), COPY)

        def fetch_both(half, t):
            fetch_n1(half, t)
            fetch_n2(half, t)

        def make_pa(half, t):
            own = h_rows[t][:, HALVES[half]]
            if (half, t) in at_n1:
                nc.vector.tensor_tensor(pa[half][:, t, :], own, at_n1[half, t][:], ALU.subtract)
            else:
                nc.vector.tensor_tensor(pa[half][:, t, :], minus_h[:].indirect(entries(n1_list, HALVES[half])), own, ALU.add)

        def make_pb(half, t):
            cols = HALVES[half]
            if (half, t) in at_n2:
                nc.vector.tensor_tensor(pb[half][:, t, :], at_n2[half, t][:], h_rows[t][:, cols], ALU.subtract)
            else:
                nc.vector.tensor_tensor(pb[half][:, t, :], h_rows[t][:].indirect(entries(n2_list, cols)), minus_h[:, cols], ALU.add)

        def differences(half, t):
            make_pa(half, t)
            make_pb(half, t)

        def cap(half, u, cols):
            pair = slice(2 * u, 2 * u + 2)
            nc.vector.scalar_tensor_tensor(
                capped[half][:, pair, cols], pb[half][:, pair, cols], 0.0, pa[half][:, pair, cols], ALU.max, ALU.min
            )

        def minmod(half, u, cols):
            pair = slice(2 * u, 2 * u + 2)
            nc.vector.scalar_tensor_tensor(
                z_pairs[half][:, u, cols, :], pb[half][:, pair, cols].rearrange("p e c -> p c e"), 0.0,
                capped[half][:, pair, cols].rearrange("p e c -> p c e"), ALU.min, ALU.max,
            )

        def open_sums(half):
            cols = HALVES[half]
            for t in range(PACK):
                h2_banks[half, t] = bank("h2_bank%d_%d" % (half, t), half, t)
                multiply(h2_banks[half, t][:], t, w2_codes, w_plane[4:P, :], two_codes[:, cols], two_plane[:, cols], True, False)

        def add_w1(half, t, cols):
            multiply(
                h2_banks[half, t][:, cols], t, w1_codes, w_plane, z_codes[half][:, cols], z_plane[half][:, cols],
                False, cols.stop == HALF,
            )

        empty_h(0)
        empty_h(1)
        fetch_both(0, 1)
        fetch_n2(1, 0)
        fetch_both(1, 1)
        empty_h(2)
        empty_h(3)
        for half in range(2):
            fetch_both(half, 2)
            fetch_both(half, 3)

        whole = slice(0, HALF)
        differences(0, 0)
        differences(0, 1)
        cap(0, 0, whole)
        differences(1, 0)
        minmod(0, 0, whole)
        differences(1, 1)
        deal(w2_codes[:], w_plain[:, 1, :])
        cap(1, 0, whole)
        deal(w_plane[:], w_plane_plain[:])
        open_sums(0)
        open_sums(1)
        minmod(1, 0, whole)
        deal(w1_codes[:], w_plain[:, 0, :])
        differences(0, 2)
        differences(0, 3)
        cap(0, 1, whole)
        differences(1, 2)
        minmod(0, 1, whole)
        make_pa(1, 3)
        weave(z_grouped[0][:], z_pairs[0], whole)
        make_pb(1, 3)
        quantise(z_codes[0], z_plane[0], z_grouped[0], whole)
        tile_order = (0, 1, 3, 2)
        for t in tile_order:
            add_w1(0, t, whole)
        quarters = (slice(0, HALF // 2), slice(HALF // 2, HALF))
        for cols in quarters:
            cap(1, 1, cols)
        for cols in quarters:
            minmod(1, 1, cols)
        for cols in quarters:
            weave(z_grouped[1][:], z_pairs[1], cols)
        for cols in quarters:
            quantise(z_codes[1], z_plane[1], z_grouped[1], cols)
        for tiles in (tile_order[:2], tile_order[2:]):
            for cols in quarters:
                for t in tiles:
                    add_w1(1, t, cols)

        h2_rows = [tile("h2_rows%d" % t, [P, S], F32) for t in range(PACK)]
        pull = [tile("pull%d" % t, [P, W], F32) for t in range(PACK)]
        old = tile("old", [P, W], F32)
        ra = {t: tile("ra%d" % t, [P, W], F32) for t in range(1, PACK)}
        left_pairs = tile("left_pairs", [P, 2, LEFT, 2], BF16, tag="pull2")
        right_pairs = tile("right_pairs", [P, 2, S - LEFT, 2], BF16)
        out_rows = out_0.rearrange("(p t) j -> p t j", t=PACK)

        def empty_h2(copy, half, t):
            copy(h2_rows[t][:, HALVES[half]], h2_banks[half, t][:])

        def fetch_pull(t):
            nc.scalar.activation(pull[t][:], h2_rows[t][:].indirect(n4_list[:]), COPY, scale=-0.5)

        def make_ra(t):
            nc.vector.tensor_tensor(ra[t][:], h2_rows[t][:].indirect(n3_list[:]), pull[t][:], ALU.add)

        def store_rows(t):
            nc.sync.dma_start(out=out_rows[:, t, :], in_=h2_rows[t][:])

        def scatter_on_scalar(t):
            nc.scalar.activation(h2_rows[t][:].indirect(n3_list[:]), ra[t][:], COPY)
            store_rows(t)

        def round_left(t):
            (nc.gpsimd if t < 2 else nc.vector).tensor_copy(out=left_pairs[:, t // 2, :, t % 2], in_=h2_rows[t][:, :LEFT])

        def round_right(t):
            nc.scalar.copy(out=right_pairs[:, t // 2, :, t % 2], in_=h2_rows[t][:, LEFT:])

        for t in range(PACK):
            empty_h2(nc.scalar.copy, 0, t)
        empty_h2(nc.scalar.copy, 1, 0)
        empty_h2(nc.vector.tensor_copy, 1, 1)
        fetch_pull(0)
        nc.vector.tensor_copy(old[:], h2_rows[0][:].indirect(n3_list[:]))
        fetch_pull(1)
        for cols in (slice(0, W // 2), slice(W // 2, W)):
            nc.vector.tensor_tensor(h2_rows[0][:].indirect(entries(n3_list, cols)), old[:, cols], pull[0][:, cols], ALU.add)
        store_rows(0)
        make_ra(1)
        for t in tile_order[2:]:
            empty_h2(nc.scalar.copy, 1, t)
        for t in tile_order[2:]:
            fetch_pull(t)
        scatter_on_scalar(1)
        for t in tile_order[2:]:
            make_ra(t)
        for round_part in (round_left, round_right):
            round_part(0)
            round_part(1)
        scatter_on_scalar(3)
        nc.vector.tensor_copy(h2_rows[2][:].indirect(n3_list[:]), ra[2][:])
        store_rows(2)
        round_right(3)
        round_left(3)
        round_left(2)
        round_right(2)

        out_grouped = tile("out_grouped", [P, S * PACK], BF16)
        weave(out_grouped[:, : LEFT * PACK], left_pairs, slice(0, LEFT))
        weave(out_grouped[:, LEFT * PACK :], right_pairs, slice(0, S - LEFT))
        out_codes = tile("out_codes", [P, S], U32)
        out_plane = tile("out_plane", [P, S], U8)
        for cols in (slice(0, LEFT), slice(LEFT, S)):
            quantise(out_codes, out_plane, out_grouped, cols)
            nc.sync.dma_start(out=words_of(out_1)[:, cols], in_=out_codes[:, cols].bitcast(I32))
        for q in range(QUADRANTS):
            queue = nc.scalar if q % 2 == 0 else nc.sync
            queue.dma_start(
                out=out_2[0, 4 * q : 4 * q + 4, :].bitcast(I32), in_=out_plane[32 * q : 32 * q + 4, :].bitcast(I32)
            )
